import numpy as np
import ml_dtypes


def mxq(x, axis, fmt="e4m3"):
    dtype, down = {"e4m3": (ml_dtypes.float8_e4m3fn, 7), "e5m2": (ml_dtypes.float8_e5m2, 14)}[fmt]
    v = np.moveaxis(np.asarray(x, np.float32).astype(ml_dtypes.bfloat16).astype(np.float64), axis, -1)
    blocks = v.reshape(v.shape[:-1] + (-1, 32))
    amax = np.abs(blocks).max(-1, keepdims=True)
    byte = np.maximum(np.where(amax > 0, np.frexp(amax)[1] - 1 + 127, 0) - down, 1)
    scale = np.exp2(byte - 127.0)
    codes = (blocks / scale).astype(np.float32).astype(dtype).astype(np.float64)
    return np.moveaxis((codes * scale).reshape(v.shape), -1, axis)


WIDE = False


def mx_kscale(k):
    if not WIDE:
        return np.ones(k)
    levels = np.array([10, -10, 5, -5, 0])
    if k % 512:
        return np.exp2(np.random.permutation(np.resize(levels, k // 32))).repeat(32)
    a = np.empty((k // 512, 16))
    for p in range(k // 512):
        a[p, :8] = np.random.permutation(np.resize(levels, 8))
        for g in range(8):
            far = levels[np.abs(levels - a[p, g]) >= 10]
            a[p, g + 8] = far[np.random.randint(len(far))]
    return np.exp2(a.ravel()).repeat(32)


def f64(x):
    return np.asarray(x).astype(np.float64)


def striped(idx):
    return np.tile(np.asarray(idx).reshape(-1, 16).T, (8, 1)).astype(np.uint16)


def unstriped(offs):
    return offs[:16].T.reshape(-1).astype(np.int64)


E2M1 = np.array([0.0, 0.5, 1.0, 1.5, 2.0, 3.0, 4.0, 6.0, -0.0, -0.5, -1.0, -1.5, -2.0, -3.0, -4.0, -6.0])


def pack_weight(w, fmt):
    k, n = w.shape
    w = f64(np.asarray(w, np.float32).astype(ml_dtypes.bfloat16)).reshape(k // 32, 32, n)
    amax = np.abs(w).max(1)
    if fmt == "e4m3":
        byte = np.frexp(amax)[1] - 1 + 127 - 7
    else:
        mant, ex = np.frexp(amax / 6.0)
        byte = np.where(mant > 0.5, ex, ex - 1) + 127
    byte = np.clip(np.where(amax > 0, byte, 1), 1, 254)
    scaled = (w * np.exp2(127.0 - byte)[:, None, :]).reshape(k, n).astype(np.float32)
    by_word = np.ascontiguousarray(scaled.reshape(k // 512, 128, 4, n).transpose(0, 1, 3, 2))
    if fmt == "e4m3":
        words = by_word.astype(ml_dtypes.float8_e4m3fn).view(np.uint8)
    else:
        c = by_word.astype(ml_dtypes.float4_e2m1fn).view(np.uint8) & 0xF
        words = (c[..., 0::2] | (c[..., 1::2] << 4)).reshape(k // 512, 128, 2 * n)
    return np.ascontiguousarray(words), np.ascontiguousarray(byte.astype(np.uint8).reshape(k // 512, 16, n))


def unpack_weight(words, scales, fmt):
    g, _, n = scales.shape
    words = np.ascontiguousarray(words).reshape(g, 128, n, -1)
    if fmt == "e4m3":
        vals = words.view(ml_dtypes.float8_e4m3fn).astype(np.float64)
    else:
        nib = np.empty((g, 128, n, 4), np.uint8)
        nib[..., 0::2] = words & 0xF
        nib[..., 1::2] = words >> 4
        vals = E2M1[nib]
    vals = vals * np.repeat(np.exp2(scales.astype(np.float64) - 127.0), 8, axis=1)[..., None]
    return vals.transpose(0, 1, 3, 2).reshape(g * 512, n)


def sigmoid(v):
    return 1.0 / (1.0 + np.exp(-v))


D, T, I, Q, E = 512, 2048, 512, 128, 512


def setup_inputs():
    n = np.random.standard_normal
    idx = np.random.permutation(T)[:I]
    fd = mx_kscale(D)
    fi = mx_kscale(I)
    ti = np.ones(T)
    ti[idx] = fi
    keysp = pack_weight(n((D, T)) / fd[:, None], "e4m3")
    return {
        "query": (n((D, Q)) * 0.8 / np.sqrt(D) * fd[:, None]).astype(np.float32),
        "query2": (n((D, Q)) * 0.8 / np.sqrt(D) * fd[:, None]).astype(np.float32),
        "keys_words": keysp[0],
        "keys_scales": keysp[1],
        "ba": (np.random.uniform(-1.0, 0.5, (Q, 1))).astype(np.float32),
        "bb": (np.random.uniform(-1.0, 0.5, (Q, 1))).astype(np.float32),
        "size": (np.random.uniform(0.5, 2.0, (1, I)) * fi).astype(np.float32),
        "vals": (n((E, T)) / ti).astype(np.float32),
        "offs": striped(idx),
    }


def reference(query, query2, keys_words, keys_scales, ba, bb, size, vals, offs):
    idx = unstriped(offs)
    keysu = unpack_weight(keys_words, keys_scales, "e4m3")
    queryq = mxq(f64(query), 0, "e4m3")
    keysidxg = keysu[:, idx]
    a = queryq.T @ keysidxg
    query2q = mxq(f64(query2), 0, "e4m3")
    b = query2q.T @ keysidxg
    p = sigmoid(a + f64(ba)) * sigmoid(b + f64(bb))
    w = p * f64(size) / np.sum(p, axis=1, keepdims=True)
    wt = w.T
    vt = f64(vals)[:, idx].T
    wtq = mxq(wt, 0, "e4m3")
    vtq = mxq(vt, 0, "e4m3")
    o = wtq.T @ vtq
    return o

@@ -1,0 +1,156 @@
+from contextlib import ExitStack
+
+import concourse.mybir as mybir
+from concourse.masks import make_identity
+
+F32 = mybir.dt.float32
+BF16 = mybir.dt.bfloat16
+I32 = mybir.dt.int32
+U32 = mybir.dt.uint32
+U16 = mybir.dt.uint16
+U8 = mybir.dt.uint8
+FP8X4 = mybir.dt.float8_e4m3fn_x4
+MULT = mybir.AluOpType.mult
+SIGMOID = mybir.ActivationFunctionType.Sigmoid
+
+P = 128
+PACK = 4
+T, SLOTS, Q, E = 2048, 512, 128, 512
+FLOPS = 3 * 2 * 128 * 512 * 512
+
+
+def tile_attend_bothquestions_kernel(tc, query, query2, keys_words, keys_scales, ba, bb, size, vals, offs, out):
+    nc = tc.nc
+    with ExitStack() as ctx:
+        keep = ctx.enter_context(tc.tile_pool(name="keep", bufs=1))
+        psum = ctx.enter_context(tc.psum_pool(name="psum", bufs=1))
+
+        offsets = keep.tile([P, SLOTS // 16], U16, name="offsets")
+        nc.sync.dma_start(offsets[:], offs)
+
+        scale_pool = keep.tile([P, T], U8, name="scale_pool", align_bytes=64)
+        nc.vector.memset(scale_pool[:].bitcast(I32), 0)
+        for quad in range(4):
+            nc.scalar.dma_start(
+                scale_pool[32 * quad : 32 * quad + 4, :].bitcast(I32),
+                keys_scales[0][4 * quad : 4 * quad + 4, :].bitcast(I32),
+            )
+
+        word_pool = keep.tile([P, T], U32, name="word_pool", tag="big_a")
+        nc.sync.dma_start(word_pool[:].bitcast(I32), keys_words[0].rearrange("p n t -> p (n t)").bitcast(I32))
+        raws = []
+        for name, tag, src in (("q_raw", "big_c", query), ("q2_raw", "q2_raw", query2)):
+            raw = keep.tile([P, PACK, Q], F32, name=name, tag=tag)
+            nc.sync.dma_start(raw[:], src.rearrange("(p j) q -> p j q", j=PACK))
+            raws.append(raw)
+
+        biases = []
+        for name, src in (("bias_a", ba), ("bias_b", bb)):
+            bias = keep.tile([P, 1], F32, name=name)
+            nc.gpsimd.dma_start(bias[:], src)
+            biases.append(bias)
+        size_cols = keep.tile([P, PACK], F32, name="size_cols")
+        nc.gpsimd.dma_start(size_cols[:], size.rearrange("o (p t) -> (o p) t", t=PACK))
+        ident = keep.tile([P, P], F32, name="ident")
+        make_identity(nc, ident[:])
+
+        def load_values(block, tag):
+            window = keep.tile([P, T], F32, name="vals_%d" % block, tag=tag)
+            nc.sync.dma_start(window[:], vals[block * P : (block + 1) * P, :])
+            return window
+
+        def gather_values(block, window):
+            picked = keep.tile([P, SLOTS], BF16, name="picked_%d" % block, align_bytes=64)
+            nc.vector.tensor_copy(picked[:], window[:].indirect(offsets[:]))
+            return picked
+
+        def turn(name, rows, bank_tag):
+            words = rows[:].bitcast(F32)
+            bank = psum.tile([P, 2, P], F32, name="bank_" + name, tag=bank_tag)
+            for u in range(2):
+                nc.tensor.transpose(bank[:, u, :], words[:, u : 2 * P : 2], ident[:])
+            grouped = keep.tile([P, P * PACK], BF16, name="grouped_" + name, align_bytes=64)
+            nc.scalar.copy(
+                grouped[:].bitcast(F32).rearrange("p (c u) -> p c u", u=2),
+                bank[:].rearrange("p u c -> p c u"),
+            )
+            return grouped
+
+        def quantize(name, grouped):
+            codes = keep.tile([P, P], U32, name="codes_" + name, align_bytes=64)
+            scales = keep.tile([P, P], U8, name="scales_" + name, align_bytes=64)
+            nc.vector.quantize_mx(out=codes[:].bitcast(FP8X4), scales=scales[:], in_=grouped[:])
+            return codes, scales
+
+        windows = [load_values(0, "big_b")]
+
+        key_scales = keep.tile([P, SLOTS], U8, name="key_scales", align_bytes=64)
+        nc.vector.tensor_copy(key_scales[:], scale_pool[:].indirect(offsets[:]))
+        key_words = keep.tile([P, SLOTS], U32, name="key_words", align_bytes=64)
+        nc.vector.tensor_copy(key_words[:], word_pool[:].indirect(offsets[:]))
+        windows.append(load_values(1, "big_a"))
+
+        grouped_q = []
+        for k in range(2):
+            grouped = keep.tile([P, Q * PACK], BF16, name="grouped_q%d" % k, align_bytes=64)
+            nc.scalar.copy(
+                grouped[:].rearrange("p (c i t) -> p c t i", i=4, t=PACK),
+                raws[k][:].rearrange("p t (c i) -> p c t i", i=4),
+            )
+            grouped_q.append(grouped)
+        windows.append(load_values(2, "big_c"))
+
+        gates = []
+        for k in range(2):
+            codes, scales = quantize("q%d" % k, grouped_q[k])
+            scores = psum.tile([P, SLOTS], F32, name="scores_%d" % k)
+            nc.tensor.matmul_mx(
+                out=scores[:], lhsT=codes[:].bitcast(FP8X4), lhsT_scale=scales[:],
+                rhs=key_words[:].bitcast(FP8X4), rhs_scale=key_scales[:], start=True, stop=True,
+            )
+            gate = keep.tile([P, SLOTS], F32, name="gate_%d" % k)
+            nc.scalar.activation(gate[:], scores[:], SIGMOID, bias=biases[k][:])
+            gates.append(gate)
+
+        size_rows = psum.tile([P, PACK, P], F32, name="size_rows")
+        for t in range(PACK):
+            nc.tensor.transpose(size_rows[:, t, :], size_cols[:, t : t + 1].to_broadcast([P, P]), ident[:])
+
+        picked = [gather_values(0, windows[0])]
+        windows.append(load_values(3, "big_b"))
+
+        both = keep.tile([P, SLOTS], F32, name="both")
+        total = keep.tile([P, 1], F32, name="total")
+        nc.vector.scalar_tensor_tensor(both[:], gates[0][:], 1.0, gates[1][:], MULT, MULT, accum_out=total[:])
+        inverse = keep.tile([P, 1], F32, name="inverse")
+        nc.vector.reciprocal(inverse[:], total[:])
+        weights = keep.tile([P, SLOTS], BF16, name="weights", align_bytes=64)
+        nc.vector.scalar_tensor_tensor(
+            weights[:].rearrange("q (p t) -> q p t", t=PACK),
+            both[:].rearrange("q (p t) -> q p t", t=PACK),
+            inverse[:],
+            size_rows[:].rearrange("q t p -> q p t"),
+            MULT,
+            MULT,
+        )
+        w_codes, w_scales = quantize("w", turn("w", weights, "turn_1"))
+
+        early = keep.tile([P, 3 * P], F32, name="early")
+        last = keep.tile([P, P], F32, name="last")
+        for block in range(4):
+            if block > 0:
+                picked.append(gather_values(block, windows[block]))
+            name = "v%d" % block
+            codes, scales = quantize(name, turn(name, picked[block], "turn_%d" % (block % 2)))
+            sums = psum.tile([P, P], F32, name="sums_%d" % block, tag="sums_%d" % (block % 2))
+            nc.tensor.matmul_mx(
+                out=sums[:], lhsT=w_codes[:].bitcast(FP8X4), lhsT_scale=w_scales[:],
+                rhs=codes[:].bitcast(FP8X4), rhs_scale=scales[:], start=True, stop=True,
+            )
+            if block < 3:
+                nc.scalar.copy(early[:, block * P : (block + 1) * P], sums[:])
+            else:
+                nc.scalar.copy(last[:], sums[:])
+            if block == 2:
+                nc.sync.dma_start(out[:, 0 : 3 * P], early[:])
+        nc.sync.dma_start(out[:, 3 * P :], last[:])

@@ -25,90 +25,76 @@ def tile_attend_bothquestions_kernel(tc, query, query2, keys_words, keys_scales,
         keep = ctx.enter_context(tc.tile_pool(name="keep", bufs=1))
         psum = ctx.enter_context(tc.psum_pool(name="psum", bufs=1))
 
-        offsets = keep.tile([P, SLOTS // 16], U16, name="offsets")
+        def sbuf(name, shape, dtype, slot=None):
+            return keep.tile(shape, dtype, name=name, tag=slot or name, align_bytes=64)
+
+        offsets = sbuf("offsets", [P, SLOTS // 16], U16)
         nc.sync.dma_start(offsets[:], offs)
 
-        scale_pool = keep.tile([P, T], U8, name="scale_pool", align_bytes=64)
-        nc.vector.memset(scale_pool[:].bitcast(I32), 0)
+        scale_pool = sbuf("scale_pool", [P, T], U8)
+        nc.gpsimd.memset(scale_pool[:].bitcast(I32), 0)
         for quad in range(4):
             nc.scalar.dma_start(
                 scale_pool[32 * quad : 32 * quad + 4, :].bitcast(I32),
                 keys_scales[0][4 * quad : 4 * quad + 4, :].bitcast(I32),
             )
 
-        word_pool = keep.tile([P, T], U32, name="word_pool", tag="big_a")
-        nc.sync.dma_start(word_pool[:].bitcast(I32), keys_words[0].rearrange("p n t -> p (n t)").bitcast(I32))
-        raws = []
-        for name, tag, src in (("q_raw", "big_c", query), ("q2_raw", "q2_raw", query2)):
-            raw = keep.tile([P, PACK, Q], F32, name=name, tag=tag)
-            nc.sync.dma_start(raw[:], src.rearrange("(p j) q -> p j q", j=PACK))
-            raws.append(raw)
-
         biases = []
         for name, src in (("bias_a", ba), ("bias_b", bb)):
-            bias = keep.tile([P, 1], F32, name=name)
-            nc.gpsimd.dma_start(bias[:], src)
+            bias = sbuf(name, [P, 1], F32)
+            nc.scalar.dma_start(bias[:], src)
             biases.append(bias)
-        size_cols = keep.tile([P, PACK], F32, name="size_cols")
-        nc.gpsimd.dma_start(size_cols[:], size.rearrange("o (p t) -> (o p) t", t=PACK))
-        ident = keep.tile([P, P], F32, name="ident")
-        make_identity(nc, ident[:])
 
-        def load_values(block, tag):
-            window = keep.tile([P, T], F32, name="vals_%d" % block, tag=tag)
+        raws = []
+        for k, src in enumerate((query, query2)):
+            raw = sbuf("raw_q%d" % k, [P, PACK, Q], F32)
+            nc.sync.dma_start(raw[:], src.rearrange("(p j) q -> p j q", j=PACK))
+            raws.append(raw)
+        word_pool = sbuf("word_pool", [P, T], U32)
+        nc.sync.dma_start(word_pool[:].bitcast(I32), keys_words[0].rearrange("p n t -> p (n t)").bitcast(I32))
+
+        def load_values(block):
+            window = sbuf("vals_%d" % block, [P, T], F32, "window_%d" % block)
             nc.sync.dma_start(window[:], vals[block * P : (block + 1) * P, :])
             return window
 
-        def gather_values(block, window):
-            picked = keep.tile([P, SLOTS], BF16, name="picked_%d" % block, align_bytes=64)
-            nc.vector.tensor_copy(picked[:], window[:].indirect(offsets[:]))
-            return picked
+        windows = [load_values(0)]
+        size_cols = sbuf("size_cols", [P, PACK], F32)
+        nc.sync.dma_start(size_cols[:], size.rearrange("o (p t) -> (o p) t", t=PACK))
+        windows.extend(load_values(block) for block in range(1, 4))
 
-        def turn(name, rows, bank_tag):
-            words = rows[:].bitcast(F32)
-            bank = psum.tile([P, 2, P], F32, name="bank_" + name, tag=bank_tag)
-            for u in range(2):
-                nc.tensor.transpose(bank[:, u, :], words[:, u : 2 * P : 2], ident[:])
-            grouped = keep.tile([P, P * PACK], BF16, name="grouped_" + name, align_bytes=64)
-            nc.scalar.copy(
-                grouped[:].bitcast(F32).rearrange("p (c u) -> p c u", u=2),
-                bank[:].rearrange("p u c -> p c u"),
-            )
-            return grouped
+        ident = sbuf("ident", [P, P], F32)
+        make_identity(nc, ident[:])
 
-        def quantize(name, grouped):
-            codes = keep.tile([P, P], U32, name="codes_" + name, align_bytes=64)
-            scales = keep.tile([P, P], U8, name="scales_" + name, align_bytes=64)
+        def quantize(name, grouped, slot=None):
+            width = grouped.shape[1] // PACK
+            codes = sbuf("codes_" + name, [P, width], U32, slot)
+            scales = sbuf("scales_" + name, [P, width], U8)
             nc.vector.quantize_mx(out=codes[:].bitcast(FP8X4), scales=scales[:], in_=grouped[:])
             return codes, scales
 
-        windows = [load_values(0, "big_b")]
-
-        key_scales = keep.tile([P, SLOTS], U8, name="key_scales", align_bytes=64)
-        nc.vector.tensor_copy(key_scales[:], scale_pool[:].indirect(offsets[:]))
-        key_words = keep.tile([P, SLOTS], U32, name="key_words", align_bytes=64)
-        nc.vector.tensor_copy(key_words[:], word_pool[:].indirect(offsets[:]))
-        windows.append(load_values(1, "big_a"))
-
-        grouped_q = []
+        grouped_q = sbuf("grouped_q", [P, 2 * Q * PACK], BF16)
         for k in range(2):
-            grouped = keep.tile([P, Q * PACK], BF16, name="grouped_q%d" % k, align_bytes=64)
-            nc.scalar.copy(
-                grouped[:].rearrange("p (c i t) -> p c t i", i=4, t=PACK),
+            nc.vector.tensor_copy(
+                grouped_q[:, k * Q * PACK : (k + 1) * Q * PACK].rearrange("p (c i t) -> p c t i", i=4, t=PACK),
                 raws[k][:].rearrange("p t (c i) -> p c t i", i=4),
             )
-            grouped_q.append(grouped)
-        windows.append(load_values(2, "big_c"))
+        q_codes, q_scales = quantize("q", grouped_q)
+
+        key_scales = sbuf("key_scales", [P, SLOTS], U8)
+        nc.vector.tensor_copy(key_scales[:], scale_pool[:].indirect(offsets[:]))
+        key_words = sbuf("key_words", [P, SLOTS], U32)
+        nc.vector.tensor_copy(key_words[:], word_pool[:].indirect(offsets[:]))
 
         gates = []
         for k in range(2):
-            codes, scales = quantize("q%d" % k, grouped_q[k])
-            scores = psum.tile([P, SLOTS], F32, name="scores_%d" % k)
+            scores = psum.tile([P, SLOTS], F32, name="scores_%d" % k, tag="bank_%d" % k)
             nc.tensor.matmul_mx(
-                out=scores[:], lhsT=codes[:].bitcast(FP8X4), lhsT_scale=scales[:],
+                out=scores[:],
+                lhsT=q_codes[:, k * Q : (k + 1) * Q].bitcast(FP8X4), lhsT_scale=q_scales[:, k * Q : (k + 1) * Q],
                 rhs=key_words[:].bitcast(FP8X4), rhs_scale=key_scales[:], start=True, stop=True,
             )
-            gate = keep.tile([P, SLOTS], F32, name="gate_%d" % k)
+            gate = sbuf("gate_%d" % k, [P, SLOTS], F32)
             nc.scalar.activation(gate[:], scores[:], SIGMOID, bias=biases[k][:])
             gates.append(gate)
 
@@ -116,15 +102,31 @@ def tile_attend_bothquestions_kernel(tc, query, query2, keys_words, keys_scales,
         for t in range(PACK):
             nc.tensor.transpose(size_rows[:, t, :], size_cols[:, t : t + 1].to_broadcast([P, P]), ident[:])
 
-        picked = [gather_values(0, windows[0])]
-        windows.append(load_values(3, "big_b"))
+        def turn(name, rows, bank_tag, grouped):
+            words = rows[:].bitcast(F32)
+            bank = psum.tile([P, 2, P], F32, name="turned_" + name, tag=bank_tag)
+            for u in range(2):
+                nc.tensor.transpose(bank[:, u, :], words[:, u : 2 * P : 2], ident[:])
+            nc.scalar.copy(
+                grouped.bitcast(F32).rearrange("p (c u) -> p c u", u=2),
+                bank[:].rearrange("p u c -> p c u"),
+            )
 
-        both = keep.tile([P, SLOTS], F32, name="both")
-        total = keep.tile([P, 1], F32, name="total")
+        def gather_and_turn(block, bank_tag):
+            picked = sbuf("picked_%d" % block, [P, SLOTS], BF16)
+            grouped = sbuf("grouped_%d" % block, [P, SLOTS], BF16)
+            nc.vector.tensor_copy(picked[:], windows[block][:].indirect(offsets[:]))
+            turn("v%d" % block, picked, bank_tag, grouped[:])
+            return grouped
+
+        grouped_0 = gather_and_turn(0, "bank_1")
+
+        both = sbuf("both", [P, SLOTS], F32, "window_0")
+        total = sbuf("total", [P, 1], F32)
         nc.vector.scalar_tensor_tensor(both[:], gates[0][:], 1.0, gates[1][:], MULT, MULT, accum_out=total[:])
-        inverse = keep.tile([P, 1], F32, name="inverse")
+        inverse = sbuf("inverse", [P, 1], F32)
         nc.vector.reciprocal(inverse[:], total[:])
-        weights = keep.tile([P, SLOTS], BF16, name="weights", align_bytes=64)
+        weights = sbuf("weights", [P, SLOTS], BF16)
         nc.vector.scalar_tensor_tensor(
             weights[:].rearrange("q (p t) -> q p t", t=PACK),
             both[:].rearrange("q (p t) -> q p t", t=PACK),
@@ -133,24 +135,36 @@ def tile_attend_bothquestions_kernel(tc, query, query2, keys_words, keys_scales,
             MULT,
             MULT,
         )
-        w_codes, w_scales = quantize("w", turn("w", weights, "turn_1"))
+        grouped_w = sbuf("grouped_w", [P, SLOTS], BF16)
+        turn("w", weights, "bank_0", grouped_w[:])
 
-        early = keep.tile([P, 3 * P], F32, name="early")
-        last = keep.tile([P, P], F32, name="last")
-        for block in range(4):
-            if block > 0:
-                picked.append(gather_values(block, windows[block]))
-            name = "v%d" % block
-            codes, scales = quantize(name, turn(name, picked[block], "turn_%d" % (block % 2)))
-            sums = psum.tile([P, P], F32, name="sums_%d" % block, tag="sums_%d" % (block % 2))
+        def multiply(block, codes, scales, bank_tag, result):
+            sums = psum.tile([P, P], F32, name="sums_%d" % block, tag=bank_tag)
             nc.tensor.matmul_mx(
                 out=sums[:], lhsT=w_codes[:].bitcast(FP8X4), lhsT_scale=w_scales[:],
-                rhs=codes[:].bitcast(FP8X4), rhs_scale=scales[:], start=True, stop=True,
+                rhs=codes.bitcast(FP8X4), rhs_scale=scales, start=True, stop=True,
             )
-            if block < 3:
-                nc.scalar.copy(early[:, block * P : (block + 1) * P], sums[:])
-            else:
-                nc.scalar.copy(last[:], sums[:])
-            if block == 2:
-                nc.sync.dma_start(out[:, 0 : 3 * P], early[:])
+            nc.scalar.copy(result, sums[:])
+
+        early = sbuf("early", [P, 2 * P], F32)
+        third = sbuf("third", [P, P], F32)
+        last = sbuf("last", [P, P], F32)
+
+        codes, scales = quantize("v0", grouped_0)
+        grouped_1 = gather_and_turn(1, "bank_2")
+        w_codes, w_scales = quantize("w", grouped_w, "window_1")
+        multiply(0, codes[:], scales[:], "bank_2", early[:, :P])
+
+        grouped_2 = gather_and_turn(2, "bank_3")
+        codes, scales = quantize("v1", grouped_1, "window_2")
+        multiply(1, codes[:], scales[:], "bank_3", early[:, P:])
+        nc.sync.dma_start(out[:, : 2 * P], early[:])
+
+        grouped_3 = gather_and_turn(3, "bank_4")
+        codes, scales = quantize("v2", grouped_2, "window_3")
+        multiply(2, codes[:], scales[:], "bank_4", third[:])
+        nc.sync.dma_start(out[:, 2 * P : 3 * P], third[:])
+
+        codes, scales = quantize("v3", grouped_3)
+        multiply(3, codes[:], scales[:], "bank_5", last[:])
         nc.sync.dma_start(out[:, 3 * P :], last[:])

@@ -15,7 +15,13 @@ SIGMOID = mybir.ActivationFunctionType.Sigmoid
 
 P = 128
 PACK = 4
-T, SLOTS, Q, E = 2048, 512, 128, 512
+TOKENS = 2048
+SLOTS = 512
+Q = 128
+VALUE_BLOCKS = 4
+QUADRANT = 32
+SCALE_ROWS = 4
+RUN = 4
 FLOPS = 3 * 2 * 128 * 512 * 512
 
 
@@ -29,39 +35,39 @@ def tile_attend_bothquestions_kernel(tc, query, query2, keys_words, keys_scales,
             return keep.tile(shape, dtype, name=name, tag=slot or name, align_bytes=64)
 
         offsets = sbuf("offsets", [P, SLOTS // 16], U16)
-        nc.sync.dma_start(offsets[:], offs)
 
-        scale_pool = sbuf("scale_pool", [P, T], U8)
+        scale_pool = sbuf("scale_pool", [P, TOKENS], U8)
         nc.gpsimd.memset(scale_pool[:].bitcast(I32), 0)
-        for quad in range(4):
-            nc.scalar.dma_start(
-                scale_pool[32 * quad : 32 * quad + 4, :].bitcast(I32),
-                keys_scales[0][4 * quad : 4 * quad + 4, :].bitcast(I32),
-            )
-
-        biases = []
-        for name, src in (("bias_a", ba), ("bias_b", bb)):
-            bias = sbuf(name, [P, 1], F32)
-            nc.scalar.dma_start(bias[:], src)
-            biases.append(bias)
 
         raws = []
         for k, src in enumerate((query, query2)):
             raw = sbuf("raw_q%d" % k, [P, PACK, Q], F32)
             nc.sync.dma_start(raw[:], src.rearrange("(p j) q -> p j q", j=PACK))
             raws.append(raw)
-        word_pool = sbuf("word_pool", [P, T], U32)
+        nc.sync.dma_start(offsets[:], offs)
+        for quad in range(P // QUADRANT):
+            nc.sync.dma_start(
+                scale_pool[QUADRANT * quad : QUADRANT * quad + SCALE_ROWS, :].bitcast(I32),
+                keys_scales[0][SCALE_ROWS * quad : SCALE_ROWS * (quad + 1), :].bitcast(I32),
+            )
+        word_pool = sbuf("word_pool", [P, TOKENS], U32)
         nc.sync.dma_start(word_pool[:].bitcast(I32), keys_words[0].rearrange("p n t -> p (n t)").bitcast(I32))
 
+        biases = []
+        for name, src in (("bias_a", ba), ("bias_b", bb)):
+            bias = sbuf(name, [P, 1], F32)
+            nc.sync.dma_start(bias[:], src)
+            biases.append(bias)
+
         def load_values(block):
-            window = sbuf("vals_%d" % block, [P, T], F32, "window_%d" % block)
+            window = sbuf("vals_%d" % block, [P, TOKENS], F32, "window_%d" % block)
             nc.sync.dma_start(window[:], vals[block * P : (block + 1) * P, :])
             return window
 
         windows = [load_values(0)]
         size_cols = sbuf("size_cols", [P, PACK], F32)
         nc.sync.dma_start(size_cols[:], size.rearrange("o (p t) -> (o p) t", t=PACK))
-        windows.extend(load_values(block) for block in range(1, 4))
+        windows.extend(load_values(block) for block in range(1, VALUE_BLOCKS))
 
         ident = sbuf("ident", [P, P], F32)
         make_identity(nc, ident[:])
@@ -74,10 +80,10 @@ def tile_attend_bothquestions_kernel(tc, query, query2, keys_words, keys_scales,
             return codes, scales
 
         grouped_q = sbuf("grouped_q", [P, 2 * Q * PACK], BF16)
-        for k in range(2):
-            nc.vector.tensor_copy(
-                grouped_q[:, k * Q * PACK : (k + 1) * Q * PACK].rearrange("p (c i t) -> p c t i", i=4, t=PACK),
-                raws[k][:].rearrange("p t (c i) -> p c t i", i=4),
+        for k, interleave in enumerate((nc.scalar.copy, nc.vector.tensor_copy)):
+            interleave(
+                grouped_q[:, k * Q * PACK : (k + 1) * Q * PACK].rearrange("p (c i t) -> p c t i", i=RUN, t=PACK),
+                raws[k][:].rearrange("p t (c i) -> p c t i", i=RUN),
             )
         q_codes, q_scales = quantize("q", grouped_q)
 
@@ -91,8 +97,12 @@ def tile_attend_bothquestions_kernel(tc, query, query2, keys_words, keys_scales,
             scores = psum.tile([P, SLOTS], F32, name="scores_%d" % k, tag="bank_%d" % k)
             nc.tensor.matmul_mx(
                 out=scores[:],
-                lhsT=q_codes[:, k * Q : (k + 1) * Q].bitcast(FP8X4), lhsT_scale=q_scales[:, k * Q : (k + 1) * Q],
-                rhs=key_words[:].bitcast(FP8X4), rhs_scale=key_scales[:], start=True, stop=True,
+                lhsT=q_codes[:, k * Q : (k + 1) * Q].bitcast(FP8X4),
+                lhsT_scale=q_scales[:, k * Q : (k + 1) * Q],
+                rhs=key_words[:].bitcast(FP8X4),
+                rhs_scale=key_scales[:],
+                start=True,
+                stop=True,
             )
             gate = sbuf("gate_%d" % k, [P, SLOTS], F32)
             nc.scalar.activation(gate[:], scores[:], SIGMOID, bias=biases[k][:])
@@ -112,14 +122,13 @@ def tile_attend_bothquestions_kernel(tc, query, query2, keys_words, keys_scales,
                 bank[:].rearrange("p u c -> p c u"),
             )
 
-        def gather_and_turn(block, bank_tag):
-            picked = sbuf("picked_%d" % block, [P, SLOTS], BF16)
-            grouped = sbuf("grouped_%d" % block, [P, SLOTS], BF16)
+        def gather_and_turn(block, slot, bank_tag, grouped):
+            picked = sbuf("picked_%d" % block, [P, SLOTS], BF16, slot)
             nc.vector.tensor_copy(picked[:], windows[block][:].indirect(offsets[:]))
-            turn("v%d" % block, picked, bank_tag, grouped[:])
-            return grouped
+            turn("v%d" % block, picked, bank_tag, grouped)
 
-        grouped_0 = gather_and_turn(0, "bank_1")
+        grouped_w0 = sbuf("grouped_w0", [P, 2 * SLOTS], BF16)
+        gather_and_turn(0, None, "bank_1", grouped_w0[:, SLOTS:])
 
         both = sbuf("both", [P, SLOTS], F32, "window_0")
         total = sbuf("total", [P, 1], F32)
@@ -135,36 +144,39 @@ def tile_attend_bothquestions_kernel(tc, query, query2, keys_words, keys_scales,
             MULT,
             MULT,
         )
-        grouped_w = sbuf("grouped_w", [P, SLOTS], BF16)
-        turn("w", weights, "bank_0", grouped_w[:])
+        turn("w", weights, "bank_0", grouped_w0[:, :SLOTS])
 
-        def multiply(block, codes, scales, bank_tag, result):
-            sums = psum.tile([P, P], F32, name="sums_%d" % block, tag=bank_tag)
+        def multiply(name, codes, scales, bank_tag, result):
+            sums = psum.tile([P, codes.shape[1]], F32, name="sums_" + name, tag=bank_tag)
             nc.tensor.matmul_mx(
-                out=sums[:], lhsT=w_codes[:].bitcast(FP8X4), lhsT_scale=w_scales[:],
-                rhs=codes.bitcast(FP8X4), rhs_scale=scales, start=True, stop=True,
+                out=sums[:],
+                lhsT=codes_w0[:, :Q].bitcast(FP8X4),
+                lhsT_scale=scales_w0[:, :Q],
+                rhs=codes.bitcast(FP8X4),
+                rhs_scale=scales,
+                start=True,
+                stop=True,
             )
             nc.scalar.copy(result, sums[:])
 
-        early = sbuf("early", [P, 2 * P], F32)
-        third = sbuf("third", [P, P], F32)
-        last = sbuf("last", [P, P], F32)
+        out_0 = sbuf("out_0", [P, P], F32)
+        out_12 = sbuf("out_12", [P, 2 * P], F32)
+        out_3 = sbuf("out_3", [P, P], F32)
 
-        codes, scales = quantize("v0", grouped_0)
-        grouped_1 = gather_and_turn(1, "bank_2")
-        w_codes, w_scales = quantize("w", grouped_w, "window_1")
-        multiply(0, codes[:], scales[:], "bank_2", early[:, :P])
+        grouped_12 = sbuf("grouped_12", [P, 2 * SLOTS], BF16)
+        gather_and_turn(1, "gate_0", "bank_2", grouped_12[:, :SLOTS])
+        codes_w0, scales_w0 = quantize("w0", grouped_w0, "window_1")
+        multiply("0", codes_w0[:, Q:], scales_w0[:, Q:], "bank_1", out_0[:])
+        nc.sync.dma_start(out[:, :P], out_0[:])
 
-        grouped_2 = gather_and_turn(2, "bank_3")
-        codes, scales = quantize("v1", grouped_1, "window_2")
-        multiply(1, codes[:], scales[:], "bank_3", early[:, P:])
-        nc.sync.dma_start(out[:, : 2 * P], early[:])
+        gather_and_turn(2, "window_0", "bank_3", grouped_12[:, SLOTS:])
 
-        grouped_3 = gather_and_turn(3, "bank_4")
-        codes, scales = quantize("v2", grouped_2, "window_3")
-        multiply(2, codes[:], scales[:], "bank_4", third[:])
-        nc.sync.dma_start(out[:, 2 * P : 3 * P], third[:])
+        grouped_3 = sbuf("grouped_3", [P, SLOTS], BF16)
+        gather_and_turn(3, "grouped_w0", "bank_4", grouped_3[:])
+        codes_12, scales_12 = quantize("v12", grouped_12, "window_3")
+        multiply("12", codes_12[:], scales_12[:], "bank_2", out_12[:])
+        nc.sync.dma_start(out[:, P : 3 * P], out_12[:])
 
-        codes, scales = quantize("v3", grouped_3)
-        multiply(3, codes[:], scales[:], "bank_5", last[:])
-        nc.sync.dma_start(out[:, 3 * P :], last[:])
+        codes_3, scales_3 = quantize("v3", grouped_3)
+        multiply("3", codes_3[:], scales_3[:], "bank_5", out_3[:])
+        nc.sync.dma_start(out[:, 3 * P :], out_3[:])

from contextlib import ExitStack

import concourse.mybir as mybir
from concourse.masks import make_identity

F32 = mybir.dt.float32
BF16 = mybir.dt.bfloat16
I32 = mybir.dt.int32
U32 = mybir.dt.uint32
U16 = mybir.dt.uint16
U8 = mybir.dt.uint8
FP8X4 = mybir.dt.float8_e4m3fn_x4
MULT = mybir.AluOpType.mult
SIGMOID = mybir.ActivationFunctionType.Sigmoid

P = 128
PACK = 4
TOKENS = 2048
SLOTS = 512
Q = 128
VALUE_BLOCKS = 4
QUADRANT = 32
SCALE_ROWS = 4
RUN = 4
FLOPS = 3 * 2 * 128 * 512 * 512


def tile_attend_bothquestions_kernel(tc, query, query2, keys_words, keys_scales, ba, bb, size, vals, offs, out):
    nc = tc.nc
    with ExitStack() as ctx:
        keep = ctx.enter_context(tc.tile_pool(name="keep", bufs=1))
        psum = ctx.enter_context(tc.psum_pool(name="psum", bufs=1))

        def sbuf(name, shape, dtype, slot=None):
            return keep.tile(shape, dtype, name=name, tag=slot or name, align_bytes=64)

        offsets = sbuf("offsets", [P, SLOTS // 16], U16)

        scale_pool = sbuf("scale_pool", [P, TOKENS], U8)
        nc.gpsimd.memset(scale_pool[:].bitcast(I32), 0)

        raws = []
        for k, src in enumerate((query, query2)):
            raw = sbuf("raw_q%d" % k, [P, PACK, Q], F32)
            nc.sync.dma_start(raw[:], src.rearrange("(p j) q -> p j q", j=PACK))
            raws.append(raw)
        nc.sync.dma_start(offsets[:], offs)
        for quad in range(P // QUADRANT):
            nc.sync.dma_start(
                scale_pool[QUADRANT * quad : QUADRANT * quad + SCALE_ROWS, :].bitcast(I32),
                keys_scales[0][SCALE_ROWS * quad : SCALE_ROWS * (quad + 1), :].bitcast(I32),
            )
        word_pool = sbuf("word_pool", [P, TOKENS], U32)
        nc.sync.dma_start(word_pool[:].bitcast(I32), keys_words[0].rearrange("p n t -> p (n t)").bitcast(I32))

        biases = []
        for name, src in (("bias_a", ba), ("bias_b", bb)):
            bias = sbuf(name, [P, 1], F32)
            nc.sync.dma_start(bias[:], src)
            biases.append(bias)

        def load_values(block):
            window = sbuf("vals_%d" % block, [P, TOKENS], F32, "window_%d" % block)
            nc.sync.dma_start(window[:], vals[block * P : (block + 1) * P, :])
            return window

        windows = [load_values(0)]
        size_cols = sbuf("size_cols", [P, PACK], F32)
        nc.sync.dma_start(size_cols[:], size.rearrange("o (p t) -> (o p) t", t=PACK))
        windows.extend(load_values(block) for block in range(1, VALUE_BLOCKS))

        ident = sbuf("ident", [P, P], F32)
        make_identity(nc, ident[:])

        def quantize(name, grouped, slot=None):
            width = grouped.shape[1] // PACK
            codes = sbuf("codes_" + name, [P, width], U32, slot)
            scales = sbuf("scales_" + name, [P, width], U8)
            nc.vector.quantize_mx(out=codes[:].bitcast(FP8X4), scales=scales[:], in_=grouped[:])
            return codes, scales

        grouped_q = sbuf("grouped_q", [P, 2 * Q * PACK], BF16)
        for k, interleave in enumerate((nc.scalar.copy, nc.vector.tensor_copy)):
            interleave(
                grouped_q[:, k * Q * PACK : (k + 1) * Q * PACK].rearrange("p (c i t) -> p c t i", i=RUN, t=PACK),
                raws[k][:].rearrange("p t (c i) -> p c t i", i=RUN),
            )
        q_codes, q_scales = quantize("q", grouped_q)

        key_scales = sbuf("key_scales", [P, SLOTS], U8)
        nc.vector.tensor_copy(key_scales[:], scale_pool[:].indirect(offsets[:]))
        key_words = sbuf("key_words", [P, SLOTS], U32)
        nc.vector.tensor_copy(key_words[:], word_pool[:].indirect(offsets[:]))

        gates = []
        for k in range(2):
            scores = psum.tile([P, SLOTS], F32, name="scores_%d" % k, tag="bank_%d" % k)
            nc.tensor.matmul_mx(
                out=scores[:],
                lhsT=q_codes[:, k * Q : (k + 1) * Q].bitcast(FP8X4),
                lhsT_scale=q_scales[:, k * Q : (k + 1) * Q],
                rhs=key_words[:].bitcast(FP8X4),
                rhs_scale=key_scales[:],
                start=True,
                stop=True,
            )
            gate = sbuf("gate_%d" % k, [P, SLOTS], F32)
            nc.scalar.activation(gate[:], scores[:], SIGMOID, bias=biases[k][:])
            gates.append(gate)

        size_rows = psum.tile([P, PACK, P], F32, name="size_rows")
        for t in range(PACK):
            nc.tensor.transpose(size_rows[:, t, :], size_cols[:, t : t + 1].to_broadcast([P, P]), ident[:])

        def turn(name, rows, bank_tag, grouped):
            words = rows[:].bitcast(F32)
            bank = psum.tile([P, 2, P], F32, name="turned_" + name, tag=bank_tag)
            for u in range(2):
                nc.tensor.transpose(bank[:, u, :], words[:, u : 2 * P : 2], ident[:])
            nc.scalar.copy(
                grouped.bitcast(F32).rearrange("p (c u) -> p c u", u=2),
                bank[:].rearrange("p u c -> p c u"),
            )

        def gather_and_turn(block, slot, bank_tag, grouped):
            picked = sbuf("picked_%d" % block, [P, SLOTS], BF16, slot)
            nc.vector.tensor_copy(picked[:], windows[block][:].indirect(offsets[:]))
            turn("v%d" % block, picked, bank_tag, grouped)

        grouped_w0 = sbuf("grouped_w0", [P, 2 * SLOTS], BF16)
        gather_and_turn(0, None, "bank_1", grouped_w0[:, SLOTS:])

        both = sbuf("both", [P, SLOTS], F32, "window_0")
        total = sbuf("total", [P, 1], F32)
        nc.vector.scalar_tensor_tensor(both[:], gates[0][:], 1.0, gates[1][:], MULT, MULT, accum_out=total[:])
        inverse = sbuf("inverse", [P, 1], F32)
        nc.vector.reciprocal(inverse[:], total[:])
        weights = sbuf("weights", [P, SLOTS], BF16)
        nc.vector.scalar_tensor_tensor(
            weights[:].rearrange("q (p t) -> q p t", t=PACK),
            both[:].rearrange("q (p t) -> q p t", t=PACK),
            inverse[:],
            size_rows[:].rearrange("q t p -> q p t"),
            MULT,
            MULT,
        )
        turn("w", weights, "bank_0", grouped_w0[:, :SLOTS])

        def multiply(name, codes, scales, bank_tag, result):
            sums = psum.tile([P, codes.shape[1]], F32, name="sums_" + name, tag=bank_tag)
            nc.tensor.matmul_mx(
                out=sums[:],
                lhsT=codes_w0[:, :Q].bitcast(FP8X4),
                lhsT_scale=scales_w0[:, :Q],
                rhs=codes.bitcast(FP8X4),
                rhs_scale=scales,
                start=True,
                stop=True,
            )
            nc.scalar.copy(result, sums[:])

        out_0 = sbuf("out_0", [P, P], F32)
        out_12 = sbuf("out_12", [P, 2 * P], F32)
        out_3 = sbuf("out_3", [P, P], F32)

        grouped_12 = sbuf("grouped_12", [P, 2 * SLOTS], BF16)
        gather_and_turn(1, "gate_0", "bank_2", grouped_12[:, :SLOTS])
        codes_w0, scales_w0 = quantize("w0", grouped_w0, "window_1")
        multiply("0", codes_w0[:, Q:], scales_w0[:, Q:], "bank_1", out_0[:])
        nc.sync.dma_start(out[:, :P], out_0[:])

        gather_and_turn(2, "window_0", "bank_3", grouped_12[:, SLOTS:])

        grouped_3 = sbuf("grouped_3", [P, SLOTS], BF16)
        gather_and_turn(3, "grouped_w0", "bank_4", grouped_3[:])
        codes_12, scales_12 = quantize("v12", grouped_12, "window_3")
        multiply("12", codes_12[:], scales_12[:], "bank_2", out_12[:])
        nc.sync.dma_start(out[:, P : 3 * P], out_12[:])

        codes_3, scales_3 = quantize("v3", grouped_3)
        multiply("3", codes_3[:], scales_3[:], "bank_5", out_3[:])
        nc.sync.dma_start(out[:, 3 * P :], out_3[:])
